import numpy as np
import ml_dtypes


def mxq(x, axis, fmt="e4m3"):
    dtype, down = {"e4m3": (ml_dtypes.float8_e4m3fn, 7), "e5m2": (ml_dtypes.float8_e5m2, 14)}[fmt]
    v = np.moveaxis(np.asarray(x, np.float32).astype(ml_dtypes.bfloat16).astype(np.float64), axis, -1)
    blocks = v.reshape(v.shape[:-1] + (-1, 32))
    amax = np.abs(blocks).max(-1, keepdims=True)
    byte = np.maximum(np.where(amax > 0, np.frexp(amax)[1] - 1 + 127, 0) - down, 1)
    scale = np.exp2(byte - 127.0)
    codes = (blocks / scale).astype(np.float32).astype(dtype).astype(np.float64)
    return np.moveaxis((codes * scale).reshape(v.shape), -1, axis)


WIDE = False


def mx_kscale(k):
    if not WIDE:
        return np.ones(k)
    levels = np.array([10, -10, 5, -5, 0])
    if k % 512:
        return np.exp2(np.random.permutation(np.resize(levels, k // 32))).repeat(32)
    a = np.empty((k // 512, 16))
    for p in range(k // 512):
        a[p, :8] = np.random.permutation(np.resize(levels, 8))
        for g in range(8):
            far = levels[np.abs(levels - a[p, g]) >= 10]
            a[p, g + 8] = far[np.random.randint(len(far))]
    return np.exp2(a.ravel()).repeat(32)


def f64(x):
    return np.asarray(x).astype(np.float64)


def striped(idx):
    return np.tile(idx.reshape(-1, 16).T, (8, 1)).astype(np.uint16)


def unstriped(offs):
    return offs[:16].T.reshape(-1).astype(np.int64)


def striped8(idx):
    return np.concatenate([x.reshape(-1, 16).T for x in idx]).astype(np.uint16)


def runs(offs, k):
    lists = np.stack([offs[16 * r : 16 * r + 16].T.reshape(-1) for r in range(8)]).astype(np.int64)
    return lists[np.arange(k) % 512 // 64]


def pack_weight(w):
    k, n = w.shape
    w = f64(np.asarray(w, np.float32).astype(ml_dtypes.bfloat16)).reshape(k // 32, 32, n)
    amax = np.abs(w).max(1)
    byte = np.clip(np.where(amax > 0, np.frexp(amax)[1] - 1 + 127 - 7, 1), 1, 254)
    scaled = (w * np.exp2(127.0 - byte)[:, None, :]).reshape(k, n).astype(np.float32)
    words = np.ascontiguousarray(scaled.reshape(k // 512, 128, 4, n).transpose(0, 1, 3, 2)).astype(ml_dtypes.float8_e4m3fn).view(np.uint8)
    return words, np.ascontiguousarray(byte.astype(np.uint8).reshape(k // 512, 16, n))


def unpack_weight(words, scales):
    g, p, n, _ = words.shape
    vals = np.ascontiguousarray(words).view(ml_dtypes.float8_e4m3fn).astype(np.float64) * np.repeat(np.exp2(scales.astype(np.float64) - 127.0), 8, axis=1)[..., None]
    return vals.transpose(0, 1, 3, 2).reshape(g * 512, n)


E2M1 = np.array([0.0, 0.5, 1.0, 1.5, 2.0, 3.0, 4.0, 6.0, -0.0, -0.5, -1.0, -1.5, -2.0, -3.0, -4.0, -6.0])


def pack_fp4(w):
    k, n = w.shape
    w = f64(np.asarray(w, np.float32).astype(ml_dtypes.bfloat16)).reshape(k // 32, 32, n)
    amax = np.abs(w).max(1)
    mant, ex = np.frexp(amax / 6.0)
    byte = np.clip(np.where(amax > 0, np.where(mant > 0.5, ex, ex - 1) + 127, 1), 1, 254)
    scaled = (w * np.exp2(127.0 - byte)[:, None, :]).reshape(k, n).astype(np.float32)
    c = np.ascontiguousarray(scaled.reshape(k // 512, 128, 4, n).transpose(0, 1, 3, 2)).astype(ml_dtypes.float4_e2m1fn).view(np.uint8) & 0xF
    words = (c[..., 0::2] | (c[..., 1::2] << 4)).reshape(k // 512, 128, 2 * n)
    return np.ascontiguousarray(words), np.ascontiguousarray(byte.astype(np.uint8).reshape(k // 512, 16, n))


def unpack_fp4(words, scales):
    g, _, n = scales.shape
    words = np.ascontiguousarray(words).reshape(g, 128, n, 2)
    nib = np.empty((g, 128, n, 4), np.uint8)
    nib[..., 0::2] = words & 0xF
    nib[..., 1::2] = words >> 4
    vals = E2M1[nib] * np.repeat(np.exp2(scales.astype(np.float64) - 127.0), 8, axis=1)[..., None]
    return vals.transpose(0, 1, 3, 2).reshape(g * 512, n)


def sigmoid(v):
    return 1.0 / (1.0 + np.exp(-np.maximum(v, -700.0)))

def planes(y):
    n, m = y.shape
    v = y.astype(np.float32).astype(ml_dtypes.bfloat16).astype(np.float64).reshape(n // 32, 32, m)
    top = np.abs(v).max(1)
    byte = np.clip(np.where(top > 0, np.frexp(top)[1] - 1 + 127 - 7, 1), 1, 254)
    codes = (v * np.exp2(127.0 - byte)[:, None, :]).reshape(n, m).astype(np.float32).astype(ml_dtypes.float8_e4m3fn).view(np.uint8)
    words = codes.reshape(n // 512, 128, 4, m).transpose(0, 1, 3, 2)
    return np.ascontiguousarray(words), np.ascontiguousarray(byte.astype(np.uint8).reshape(n // 512, 16, m))


K, T, S, H, W = 512, 2048, 256, 512, 128


def setup_inputs():
    n = np.random.standard_normal
    s = mx_kscale(K)[:, None]
    u = mx_kscale(H)
    packed_xT = pack_weight(n((K, T)) * s)
    packed_w1 = pack_fp4(n((K, H)) / np.sqrt(K) / s)
    packed_w2 = pack_fp4(n((H, H)) / np.sqrt(H) / u[:, None])
    perm = np.random.permutation(S)
    return {
        "x_words": packed_xT[0],
        "x_scales": packed_xT[1],
        "w1_words": packed_w1[0],
        "w1_scales": packed_w1[1],
        "gn": (np.random.uniform(0.5, 1.5, (H, 1)) * u[:, None]).astype(np.float32),
        "w2_words": packed_w2[0],
        "w2_scales": packed_w2[1],
        "offs": striped(np.random.permutation(T)[:S]),
        "n1": striped(perm[:W]),
        "n2": striped(perm[W:]),
        "n3": striped8(np.stack([np.random.permutation(S) for _ in range(8)])),
        "n4": striped8(np.stack([np.random.permutation(S) for _ in range(8)])),
        "n5": striped8(np.stack([np.random.permutation(S) for _ in range(8)])),
        "n6": striped8(np.stack([np.random.permutation(S) for _ in range(8)])),
    }


def reference(x_words, x_scales, w1_words, w1_scales, gn, w2_words, w2_scales, offs, n1, n2, n3, n4, n5, n6):
    xq = unpack_weight(x_words, x_scales)[:, unstriped(offs)]
    y = unpack_fp4(w1_words, w1_scales).T @ xq
    pa = y[:, unstriped(n1)]
    pb = y[:, unstriped(n2)]
    rb = pa * pb
    ra = pa + pb
    ds = np.zeros((H, S))
    ds[:, unstriped(n1)] = ra
    dt = ds.copy()
    dt[:, unstriped(n2)] = rb
    z = f64(gn) * dt
    w2q = unpack_fp4(w2_words, w2_scales)
    a = w2q.T @ mxq(z, 0, "e4m3")
    z2 = f64(gn) * (0.75 * (y[np.arange(H)[:, None], runs(n3, H)] + y[np.arange(H)[:, None], runs(n4, H)]) - y)
    b = w2q.T @ mxq(z2, 0, "e4m3")
    out_0 = (a + a[np.arange(H)[:, None], runs(n5, H)]) * (sigmoid(b + b[np.arange(H)[:, None], runs(n6, H)]))
    return (out_0,) + planes(out_0)

@@ -1,0 +1,182 @@
+from contextlib import ExitStack
+
+import concourse.mybir as mybir
+
+T, S, H, W = 2048, 256, 512, 128
+P = 128
+PACK = 4
+WINDOW = 2 * S
+HALF = S // 2
+X_SPLIT = 768
+FLOPS = 3 * 2 * H * H * S
+
+F32 = mybir.dt.float32
+BF16 = mybir.dt.bfloat16
+I32 = mybir.dt.int32
+U32 = mybir.dt.uint32
+U16 = mybir.dt.uint16
+U8 = mybir.dt.uint8
+FP8X4 = mybir.dt.float8_e4m3fn_x4
+FP4X4 = mybir.dt.float4_e2m1fn_x4
+ALU = mybir.AluOpType
+ACT = mybir.ActivationFunctionType
+
+
+def tile_picked_tietriebbondlap_none_po_kernel(tc, x_words, x_scales, w1_words, w1_scales, gn, w2_words, w2_scales,
+        offs, n1, n2, n3, n4, n5, n6, out_0, out_1, out_2):
+    nc = tc.nc
+    with ExitStack() as ctx:
+        pool = ctx.enter_context(tc.tile_pool(name="sbuf", bufs=1))
+        psum = ctx.enter_context(tc.psum_pool(name="psum", bufs=1))
+
+        def load_list(name, src):
+            tl = pool.tile(list(src.shape), U16, name=name)
+            nc.sync.dma_start(tl[:], src)
+            return tl
+
+        def zeroed_plane(name, width):
+            tl = pool.tile([P, width], U8, name=name, align_bytes=64)
+            nc.vector.memset(tl[:].bitcast(I32), 0)
+            return tl
+
+        def load_scale_rows(eng, tl, src):
+            for q in range(4):
+                eng.dma_start(tl[32 * q : 32 * q + 4, :].bitcast(I32), src[0, 4 * q : 4 * q + 4, :].bitcast(I32))
+
+        def deal_words(raw):
+            dealt = pool.tile([P, 2 * H], U8, name="dealt_words", align_bytes=64)
+            nc.vector.tensor_copy(dealt[:].rearrange("p (t m e) -> p t m e", t=PACK, e=2),
+                                  raw[:].rearrange("p (m t e) -> p t m e", t=PACK, e=2))
+            return dealt
+
+        def deal_scales(raw):
+            dealt = pool.tile([P, H], U8, name="dealt_scales", align_bytes=64)
+            nc.vector.tensor_copy(dealt[:].rearrange("p (t m) -> p t m", t=PACK),
+                                  raw[:].rearrange("p (m t) -> p t m", t=PACK))
+            return dealt
+
+        ws_raw = zeroed_plane("ws_raw", H)
+        xs_all = zeroed_plane("xs_all", T)
+        ww_raw = pool.tile([P, 2 * H], U8, name="ww_raw", align_bytes=64)
+
+        offs_t = load_list("offs_t", offs)
+        nc.sync.dma_start(ww_raw[:].bitcast(I32), w1_words[0].bitcast(I32))
+        load_scale_rows(nc.sync, ws_raw, w1_scales)
+        xw_all = pool.tile([P, T], I32, name="xw_all", align_bytes=64)
+        x_rows = x_words[0].rearrange("p c r -> p (c r)").bitcast(I32)
+        nc.scalar.dma_start(xw_all[:, :X_SPLIT], x_rows[:, :X_SPLIT])
+        nc.gpsimd.dma_start(xw_all[:, X_SPLIT:], x_rows[:, X_SPLIT:])
+        load_scale_rows(nc.sync, xs_all, x_scales)
+        n1_t = load_list("n1_t", n1)
+        n2_t = load_list("n2_t", n2)
+        n3_t = load_list("n3_t", n3)
+        n4_t = load_list("n4_t", n4)
+        gain = pool.tile([P, PACK], F32, name="gain")
+        nc.sync.dma_start(gain[:], gn.rearrange("(p t) o -> p (t o)", t=PACK))
+        n6_t = load_list("n6_t", n6)
+        n5_t = load_list("n5_t", n5)
+
+        w1w = deal_words(ww_raw)
+        w1s = deal_scales(ws_raw)
+        nc.sync.dma_start(ww_raw[:].bitcast(I32), w2_words[0].bitcast(I32))
+        load_scale_rows(nc.sync, ws_raw, w2_scales)
+
+        xs = pool.tile([P, S], U8, name="xs", align_bytes=64)
+        nc.vector.tensor_copy(xs[:], xs_all[:].indirect(offs_t[:]))
+        xw = pool.tile([P, S], U32, name="xw", align_bytes=64)
+        nc.vector.tensor_copy(xw[:], xw_all[:].bitcast(U32).indirect(offs_t[:]))
+
+        def product(name, bank0, factor, words, scales, codes, code_scales):
+            res = []
+            for t in range(PACK):
+                acc = psum.tile([P, S], F32, name="acc", tag="bank%d" % (bank0 + t))
+                nc.tensor.matmul_mx(
+                    out=acc[:],
+                    lhsT=words[:, 2 * P * t : 2 * P * (t + 1)].bitcast(FP4X4),
+                    lhsT_scale=scales[:, P * t : P * (t + 1)],
+                    rhs=codes[:].bitcast(FP8X4),
+                    rhs_scale=code_scales[:],
+                    start=True, stop=True)
+                win = pool.tile([P, WINDOW], F32, name="%s%d" % (name, t))
+                nc.vector.tensor_scalar(win[:, :S], acc[:], factor, None, ALU.mult)
+                res.append(win)
+            return res
+
+        def fetch(dst, win, lst):
+            nc.scalar.activation(dst, win[:].indirect(lst), ACT.Copy)
+
+        def quantize(name, grouped, tag):
+            codes = pool.tile([P, S], U32, name=name + "_codes", tag=tag, align_bytes=64)
+            scales = pool.tile([P, S], U8, name=name + "_scales", align_bytes=64)
+            nc.vector.quantize_mx(out=codes[:].bitcast(FP8X4), scales=scales[:],
+                                  in_=grouped[:].rearrange("p c t -> p (c t)"))
+            return codes, scales
+
+        y = product("y", 0, 1.0, w1w, w1s, xw, xs)
+
+        ra, rb = [], []
+        for t in range(PACK):
+            pa = pool.tile([P, W], F32, name="pa%d" % t)
+            pb = pool.tile([P, W], F32, name="pb%d" % t)
+            fetch(pa[:], y[t], n1_t[:])
+            fetch(pb[:], y[t], n2_t[:])
+            ra.append(pool.tile([P, W], F32, name="ra%d" % t))
+            rb.append(pool.tile([P, W], F32, name="rb%d" % t))
+            nc.vector.tensor_tensor(ra[t][:], pa[:], pb[:], ALU.add)
+            nc.vector.tensor_tensor(rb[t][:], pa[:], pb[:], ALU.mult)
+
+        w2w = deal_words(ww_raw)
+        w2s = deal_scales(ws_raw)
+
+        z2 = pool.tile([P, S, PACK], BF16, name="z2", align_bytes=64)
+        for t in range(PACK):
+            y3 = pool.tile([P, S], F32, name="y3_%d" % t)
+            y4 = pool.tile([P, S], F32, name="y4_%d" % t)
+            fetch(y3[:], y[t], n3_t[:])
+            fetch(y4[:], y[t], n4_t[:])
+            both = pool.tile([P, S], F32, name="both%d" % t)
+            nc.vector.tensor_tensor(both[:], y3[:], y4[:], ALU.add)
+            lap = pool.tile([P, S], F32, name="lap%d" % t)
+            nc.vector.scalar_tensor_tensor(lap[:], both[:], 0.75, y[t][:, :S], ALU.mult, ALU.subtract)
+            nc.vector.tensor_scalar(z2[:, :, t], lap[:], gain[:, t : t + 1], None, ALU.mult)
+        b = product("b", PACK, 0.5, w2w, w2s, *quantize("z2", z2, "handed_on"))
+
+        z = pool.tile([P, S, PACK], BF16, name="z", tag="handed_on", align_bytes=64)
+        for t in range(PACK):
+            dt = pool.tile([P, S], F32, name="dt%d" % t)
+            nc.scalar.activation(dt[:].indirect(n1_t[:]), ra[t][:], ACT.Copy)
+            nc.scalar.activation(dt[:].indirect(n2_t[:]), rb[t][:], ACT.Copy)
+            nc.vector.tensor_scalar(z[:, :, t], dt[:], gain[:, t : t + 1], None, ALU.mult)
+        a = product("a", 0, 0.5, w2w, w2s, *quantize("z", z, "z_codes"))
+
+        gate = pool.tile([P, PACK, S], F32, name="gate")
+        bsum = pool.tile([P, PACK, S], F32, name="bsum", tag="handed_on", align_bytes=64)
+        for t in range(PACK):
+            b6 = pool.tile([P, S], F32, name="b6_%d" % t)
+            fetch(b6[:], b[t], n6_t[:])
+            nc.vector.tensor_tensor(bsum[:, t, :], b6[:], b[t][:, :S], ALU.add)
+            nc.scalar.activation(gate[:, t, :], bsum[:, t, :], ACT.Tanh)
+
+        out_rows = out_0.rearrange("(p t) c -> p t c", t=PACK)
+        out_codes = pool.tile([P, S], U32, name="out_codes", align_bytes=64)
+        out_scales = pool.tile([P, S], U8, name="out_scales", align_bytes=64)
+        out_words = out_1[0].rearrange("p c r -> p (c r)").bitcast(I32)
+        for h in range(2):
+            cols = slice(HALF * h, HALF * (h + 1))
+            a5 = pool.tile([P, PACK, HALF], F32, name="a5", tag=("a5_first", "handed_on")[h], align_bytes=64)
+            res = pool.tile([P, PACK, HALF], F32, name="res%d" % h)
+            res_bf = pool.tile([P, HALF, PACK], BF16, name="res_bf%d" % h, align_bytes=64)
+            for t in range(PACK):
+                fetch(a5[:, t, :], a[t], n5_t[:, HALF // 16 * h : HALF // 16 * (h + 1)])
+                asum = pool.tile([P, HALF], F32, name="asum%d_%d" % (h, t))
+                nc.vector.tensor_tensor(asum[:], a5[:, t, :], a[t][:, cols], ALU.add)
+                nc.vector.scalar_tensor_tensor(res[:, t, :], gate[:, t, cols], 1.0, asum[:], ALU.add, ALU.mult)
+            nc.vector.tensor_copy(res_bf[:].rearrange("p (c i) t -> p c t i", i=4),
+                                  res[:].rearrange("p t (c i) -> p c t i", i=4))
+            nc.sync.dma_start(out_rows[:, :, cols], res[:])
+            nc.vector.quantize_mx(out=out_codes[:, cols].bitcast(FP8X4), scales=out_scales[:, cols],
+                                  in_=res_bf[:].rearrange("p c t -> p (c t)"))
+            nc.sync.dma_start(out_words[:, cols], out_codes[:, cols].bitcast(I32))
+        for q in range(4):
+            eng = nc.scalar if q % 2 == 0 else nc.sync
+            eng.dma_start(out_2[0, 4 * q : 4 * q + 4, :].bitcast(I32), out_scales[32 * q : 32 * q + 4, :].bitcast(I32))

@@ -8,6 +8,7 @@ PACK = 4
 WINDOW = 2 * S
 HALF = S // 2
 X_SPLIT = 768
+PIECES = ((0, 128), (128, 64), (192, 64))
 FLOPS = 3 * 2 * H * H * S
 
 F32 = mybir.dt.float32
@@ -39,8 +40,8 @@ def tile_picked_tietriebbondlap_none_po_kernel(tc, x_words, x_scales, w1_words, 
             nc.vector.memset(tl[:].bitcast(I32), 0)
             return tl
 
-        def load_scale_rows(eng, tl, src):
-            for q in range(4):
+        def load_scale_rows(eng, tl, src, quadrants):
+            for q in quadrants:
                 eng.dma_start(tl[32 * q : 32 * q + 4, :].bitcast(I32), src[0, 4 * q : 4 * q + 4, :].bitcast(I32))
 
         def deal_words(raw):
@@ -49,10 +50,17 @@ def tile_picked_tietriebbondlap_none_po_kernel(tc, x_words, x_scales, w1_words, 
                                   raw[:].rearrange("p (m t e) -> p t m e", t=PACK, e=2))
             return dealt
 
-        def deal_scales(raw):
+        def deal_words_on_scalar(raw):
+            dealt = pool.tile([P, 2 * H], U8, name="dealt_words", align_bytes=64)
+            nc.scalar.copy(dealt[:].bitcast(U16).rearrange("p (t m) -> p t m", t=PACK),
+                           raw[:].bitcast(U16).rearrange("p (m t) -> p t m", t=PACK))
+            return dealt
+
+        def deal_scales(raw, pieces):
             dealt = pool.tile([P, H], U8, name="dealt_scales", align_bytes=64)
-            nc.vector.tensor_copy(dealt[:].rearrange("p (t m) -> p t m", t=PACK),
-                                  raw[:].rearrange("p (m t) -> p t m", t=PACK))
+            for ts in pieces:
+                nc.vector.tensor_copy(dealt[:].rearrange("p (t m) -> p t m", t=PACK)[:, ts, :],
+                                      raw[:].rearrange("p (m t) -> p t m", t=PACK)[:, ts, :])
             return dealt
 
         ws_raw = zeroed_plane("ws_raw", H)
@@ -61,12 +69,13 @@ def tile_picked_tietriebbondlap_none_po_kernel(tc, x_words, x_scales, w1_words, 
 
         offs_t = load_list("offs_t", offs)
         nc.sync.dma_start(ww_raw[:].bitcast(I32), w1_words[0].bitcast(I32))
-        load_scale_rows(nc.sync, ws_raw, w1_scales)
+        load_scale_rows(nc.sync, ws_raw, w1_scales, range(1))
         xw_all = pool.tile([P, T], I32, name="xw_all", align_bytes=64)
         x_rows = x_words[0].rearrange("p c r -> p (c r)").bitcast(I32)
         nc.scalar.dma_start(xw_all[:, :X_SPLIT], x_rows[:, :X_SPLIT])
         nc.gpsimd.dma_start(xw_all[:, X_SPLIT:], x_rows[:, X_SPLIT:])
-        load_scale_rows(nc.sync, xs_all, x_scales)
+        load_scale_rows(nc.sync, xs_all, x_scales, range(4))
+        load_scale_rows(nc.sync, ws_raw, w1_scales, range(1, 4))
         n1_t = load_list("n1_t", n1)
         n2_t = load_list("n2_t", n2)
         n3_t = load_list("n3_t", n3)
@@ -76,15 +85,16 @@ def tile_picked_tietriebbondlap_none_po_kernel(tc, x_words, x_scales, w1_words, 
         n6_t = load_list("n6_t", n6)
         n5_t = load_list("n5_t", n5)
 
-        w1w = deal_words(ww_raw)
-        w1s = deal_scales(ws_raw)
-        nc.sync.dma_start(ww_raw[:].bitcast(I32), w2_words[0].bitcast(I32))
-        load_scale_rows(nc.sync, ws_raw, w2_scales)
+        w1w = deal_words_on_scalar(ww_raw)
 
         xs = pool.tile([P, S], U8, name="xs", align_bytes=64)
         nc.vector.tensor_copy(xs[:], xs_all[:].indirect(offs_t[:]))
-        xw = pool.tile([P, S], U32, name="xw", align_bytes=64)
+        xw = pool.tile([P, S], U32, name="xw", tag="xs_all", align_bytes=64)
         nc.vector.tensor_copy(xw[:], xw_all[:].bitcast(U32).indirect(offs_t[:]))
+
+        w1s = deal_scales(ws_raw, [slice(0, 1), slice(1, PACK)])
+        nc.sync.dma_start(ww_raw[:].bitcast(I32), w2_words[0].bitcast(I32))
+        load_scale_rows(nc.sync, ws_raw, w2_scales, range(4))
 
         def product(name, bank0, factor, words, scales, codes, code_scales):
             res = []
@@ -126,7 +136,7 @@ def tile_picked_tietriebbondlap_none_po_kernel(tc, x_words, x_scales, w1_words, 
             nc.vector.tensor_tensor(rb[t][:], pa[:], pb[:], ALU.mult)
 
         w2w = deal_words(ww_raw)
-        w2s = deal_scales(ws_raw)
+        w2s = deal_scales(ws_raw, [slice(0, PACK)])
 
         z2 = pool.tile([P, S, PACK], BF16, name="z2", align_bytes=64)
         for t in range(PACK):
@@ -142,11 +152,13 @@ def tile_picked_tietriebbondlap_none_po_kernel(tc, x_words, x_scales, w1_words, 
         b = product("b", PACK, 0.5, w2w, w2s, *quantize("z2", z2, "handed_on"))
 
         z = pool.tile([P, S, PACK], BF16, name="z", tag="handed_on", align_bytes=64)
+        dt = [pool.tile([P, S], F32, name="dt%d" % t) for t in range(PACK)]
+        nc.scalar.activation(dt[0][:].indirect(n1_t[:]), ra[0][:], ACT.Copy)
         for t in range(PACK):
-            dt = pool.tile([P, S], F32, name="dt%d" % t)
-            nc.scalar.activation(dt[:].indirect(n1_t[:]), ra[t][:], ACT.Copy)
-            nc.scalar.activation(dt[:].indirect(n2_t[:]), rb[t][:], ACT.Copy)
-            nc.vector.tensor_scalar(z[:, :, t], dt[:], gain[:, t : t + 1], None, ALU.mult)
+            if t + 1 < PACK:
+                nc.scalar.activation(dt[t + 1][:].indirect(n1_t[:]), ra[t + 1][:], ACT.Copy)
+            nc.scalar.activation(dt[t][:].indirect(n2_t[:]), rb[t][:], ACT.Copy)
+            nc.vector.tensor_scalar(z[:, :, t], dt[t][:], gain[:, t : t + 1], None, ALU.mult)
         a = product("a", 0, 0.5, w2w, w2s, *quantize("z", z, "z_codes"))
 
         gate = pool.tile([P, PACK, S], F32, name="gate")
@@ -161,22 +173,28 @@ def tile_picked_tietriebbondlap_none_po_kernel(tc, x_words, x_scales, w1_words, 
         out_codes = pool.tile([P, S], U32, name="out_codes", align_bytes=64)
         out_scales = pool.tile([P, S], U8, name="out_scales", align_bytes=64)
         out_words = out_1[0].rearrange("p c r -> p (c r)").bitcast(I32)
-        for h in range(2):
-            cols = slice(HALF * h, HALF * (h + 1))
-            a5 = pool.tile([P, PACK, HALF], F32, name="a5", tag=("a5_first", "handed_on")[h], align_bytes=64)
-            res = pool.tile([P, PACK, HALF], F32, name="res%d" % h)
-            res_bf = pool.tile([P, HALF, PACK], BF16, name="res_bf%d" % h, align_bytes=64)
+        res = pool.tile([P, PACK, S], F32, name="res")
+        a5_first = pool.tile([P, PACK, HALF], F32, name="a5_first")
+        a5_rest = pool.tile([P, PACK * HALF], F32, name="a5_rest", tag="handed_on", align_bytes=64)
+        for h, (c0, n) in enumerate(PIECES):
+            cols = slice(c0, c0 + n)
+            a5 = a5_first[:] if h == 0 else a5_rest[:, PACK * (c0 - HALF) : PACK * (c0 - HALF + n)].rearrange("p (t c) -> p t c", t=PACK)
+            res_bf = pool.tile([P, n, PACK], BF16, name="res_bf%d" % h, align_bytes=64)
             for t in range(PACK):
-                fetch(a5[:, t, :], a[t], n5_t[:, HALF // 16 * h : HALF // 16 * (h + 1)])
-                asum = pool.tile([P, HALF], F32, name="asum%d_%d" % (h, t))
+                window = a[t][:] if h == 0 else a[t][:, :S]
+                nc.scalar.activation(a5[:, t, :], window.indirect(n5_t[:, c0 // 16 : (c0 + n) // 16]), ACT.Copy)
+                asum = pool.tile([P, n], F32, name="asum%d_%d" % (h, t))
                 nc.vector.tensor_tensor(asum[:], a5[:, t, :], a[t][:, cols], ALU.add)
-                nc.vector.scalar_tensor_tensor(res[:, t, :], gate[:, t, cols], 1.0, asum[:], ALU.add, ALU.mult)
+                nc.vector.scalar_tensor_tensor(res[:, t, cols], gate[:, t, cols], 1.0, asum[:], ALU.add, ALU.mult)
             nc.vector.tensor_copy(res_bf[:].rearrange("p (c i) t -> p c t i", i=4),
-                                  res[:].rearrange("p t (c i) -> p c t i", i=4))
-            nc.sync.dma_start(out_rows[:, :, cols], res[:])
+                                  res[:, :, cols].rearrange("p t (c i) -> p c t i", i=4))
+            if h != 1:
+                half = slice(c0 + n - HALF, c0 + n)
+                nc.sync.dma_start(out_rows[:, :, half], res[:, :, half])
             nc.vector.quantize_mx(out=out_codes[:, cols].bitcast(FP8X4), scales=out_scales[:, cols],
                                   in_=res_bf[:].rearrange("p c t -> p (c t)"))
-            nc.sync.dma_start(out_words[:, cols], out_codes[:, cols].bitcast(I32))
+            if h != 1:
+                nc.sync.dma_start(out_words[:, half], out_codes[:, half].bitcast(I32))
         for q in range(4):
             eng = nc.scalar if q % 2 == 0 else nc.sync
             eng.dma_start(out_2[0, 4 * q : 4 * q + 4, :].bitcast(I32), out_scales[32 * q : 32 * q + 4, :].bitcast(I32))

@@ -8,7 +8,7 @@ PACK = 4
 WINDOW = 2 * S
 HALF = S // 2
 X_SPLIT = 768
-PIECES = ((0, 128), (128, 64), (192, 64))
+PIECES = ((0, 128), (128, 128))
 FLOPS = 3 * 2 * H * H * S
 
 F32 = mybir.dt.float32
@@ -90,7 +90,9 @@ def tile_picked_tietriebbondlap_none_po_kernel(tc, x_words, x_scales, w1_words, 
         xs = pool.tile([P, S], U8, name="xs", align_bytes=64)
         nc.vector.tensor_copy(xs[:], xs_all[:].indirect(offs_t[:]))
         xw = pool.tile([P, S], U32, name="xw", tag="xs_all", align_bytes=64)
-        nc.vector.tensor_copy(xw[:], xw_all[:].bitcast(U32).indirect(offs_t[:]))
+        for h in range(2):
+            nc.vector.tensor_copy(xw[:, HALF * h : HALF * (h + 1)],
+                                  xw_all[:].bitcast(U32).indirect(offs_t[:, HALF // 16 * h : HALF // 16 * (h + 1)]))
 
         w1s = deal_scales(ws_raw, [slice(0, 1), slice(1, PACK)])
         nc.sync.dma_start(ww_raw[:].bitcast(I32), w2_words[0].bitcast(I32))
@@ -100,13 +102,14 @@ def tile_picked_tietriebbondlap_none_po_kernel(tc, x_words, x_scales, w1_words, 
             res = []
             for t in range(PACK):
                 acc = psum.tile([P, S], F32, name="acc", tag="bank%d" % (bank0 + t))
-                nc.tensor.matmul_mx(
-                    out=acc[:],
-                    lhsT=words[:, 2 * P * t : 2 * P * (t + 1)].bitcast(FP4X4),
-                    lhsT_scale=scales[:, P * t : P * (t + 1)],
-                    rhs=codes[:].bitcast(FP8X4),
-                    rhs_scale=code_scales[:],
-                    start=True, stop=True)
+                for cols in ([slice(0, HALF), slice(HALF, S)] if (name, t) == ("y", 0) else [slice(0, S)]):
+                    nc.tensor.matmul_mx(
+                        out=acc[:, cols],
+                        lhsT=words[:, 2 * P * t : 2 * P * (t + 1)].bitcast(FP4X4),
+                        lhsT_scale=scales[:, P * t : P * (t + 1)],
+                        rhs=codes[:, cols].bitcast(FP8X4),
+                        rhs_scale=code_scales[:, cols],
+                        start=True, stop=True)
                 win = pool.tile([P, WINDOW], F32, name="%s%d" % (name, t))
                 nc.vector.tensor_scalar(win[:, :S], acc[:], factor, None, ALU.mult)
                 res.append(win)
@@ -161,13 +164,19 @@ def tile_picked_tietriebbondlap_none_po_kernel(tc, x_words, x_scales, w1_words, 
             nc.vector.tensor_scalar(z[:, :, t], dt[t][:], gain[:, t : t + 1], None, ALU.mult)
         a = product("a", 0, 0.5, w2w, w2s, *quantize("z", z, "z_codes"))
 
-        gate = pool.tile([P, PACK, S], F32, name="gate")
+        gate = {}
+
+        def make_gate(u, h, tag):
+            gate[u, h] = pool.tile([P, 2, HALF], F32, name="gate", tag=tag)
+            nc.scalar.activation(gate[u, h][:], bsum[:, 2 * u : 2 * u + 2, HALF * h : HALF * (h + 1)], ACT.Tanh)
+
         bsum = pool.tile([P, PACK, S], F32, name="bsum", tag="handed_on", align_bytes=64)
         for t in range(PACK):
             b6 = pool.tile([P, S], F32, name="b6_%d" % t)
             fetch(b6[:], b[t], n6_t[:])
             nc.vector.tensor_tensor(bsum[:, t, :], b6[:], b[t][:, :S], ALU.add)
-            nc.scalar.activation(gate[:, t, :], bsum[:, t, :], ACT.Tanh)
+            if t % 2 == 1:
+                make_gate(t // 2, 0, "gate%d" % (t // 2))
 
         out_rows = out_0.rearrange("(p t) c -> p t c", t=PACK)
         out_codes = pool.tile([P, S], U32, name="out_codes", align_bytes=64)
@@ -175,26 +184,35 @@ def tile_picked_tietriebbondlap_none_po_kernel(tc, x_words, x_scales, w1_words, 
         out_words = out_1[0].rearrange("p c r -> p (c r)").bitcast(I32)
         res = pool.tile([P, PACK, S], F32, name="res")
         a5_first = pool.tile([P, PACK, HALF], F32, name="a5_first")
-        a5_rest = pool.tile([P, PACK * HALF], F32, name="a5_rest", tag="handed_on", align_bytes=64)
+        a5_rest = pool.tile([P, PACK * HALF], F32, name="a5_rest", tag="b3")
         for h, (c0, n) in enumerate(PIECES):
             cols = slice(c0, c0 + n)
             a5 = a5_first[:] if h == 0 else a5_rest[:, PACK * (c0 - HALF) : PACK * (c0 - HALF + n)].rearrange("p (t c) -> p t c", t=PACK)
-            res_bf = pool.tile([P, n, PACK], BF16, name="res_bf%d" % h, align_bytes=64)
+            asum = pool.tile([P, PACK, n], F32, name="asum%d" % h)
             for t in range(PACK):
-                window = a[t][:] if h == 0 else a[t][:, :S]
-                nc.scalar.activation(a5[:, t, :], window.indirect(n5_t[:, c0 // 16 : (c0 + n) // 16]), ACT.Copy)
-                asum = pool.tile([P, n], F32, name="asum%d_%d" % (h, t))
-                nc.vector.tensor_tensor(asum[:], a5[:, t, :], a[t][:, cols], ALU.add)
-                nc.vector.scalar_tensor_tensor(res[:, t, cols], gate[:, t, cols], 1.0, asum[:], ALU.add, ALU.mult)
-            nc.vector.tensor_copy(res_bf[:].rearrange("p (c i) t -> p c t i", i=4),
-                                  res[:, :, cols].rearrange("p t (c i) -> p c t i", i=4))
-            if h != 1:
-                half = slice(c0 + n - HALF, c0 + n)
-                nc.sync.dma_start(out_rows[:, :, half], res[:, :, half])
-            nc.vector.quantize_mx(out=out_codes[:, cols].bitcast(FP8X4), scales=out_scales[:, cols],
-                                  in_=res_bf[:].rearrange("p c t -> p (c t)"))
-            if h != 1:
-                nc.sync.dma_start(out_words[:, half], out_codes[:, half].bitcast(I32))
+                fetch(a5[:, t, :], a[t], n5_t[:, c0 // 16 : (c0 + n) // 16])
+                nc.vector.tensor_tensor(asum[:, t, :], a5[:, t, :], a[t][:, cols], ALU.add)
+                if h == 0:
+                    nc.vector.scalar_tensor_tensor(res[:, t, cols], gate[t // 2, 0][:, t % 2, :], 1.0, asum[:, t, :], ALU.add, ALU.mult)
+            if h == 1:
+                for u in range(2):
+                    ts = slice(2 * u, 2 * u + 2)
+                    make_gate(u, 1, "a%d" % u)
+                    nc.vector.scalar_tensor_tensor(res[:, ts, cols], gate[u, 1][:], 1.0, asum[:, ts, :], ALU.add, ALU.mult)
+            nc.sync.dma_start(out_rows[:, :, cols], res[:, :, cols])
+            if h == 0:
+                shares = [(nc.vector.tensor_copy, cols)]
+            else:
+                shares = [(nc.vector.tensor_copy, slice(c0, c0 + n // 2)), (nc.scalar.copy, slice(c0 + n // 2, c0 + n))]
+            rounded = []
+            for copy, part in shares:
+                res_bf = pool.tile([P, part.stop - part.start, PACK], BF16, name="res_bf%d" % part.start, align_bytes=64)
+                copy(res_bf[:].rearrange("p (c i) t -> p c t i", i=4), res[:, :, part].rearrange("p t (c i) -> p c t i", i=4))
+                rounded.append((res_bf, part))
+            for res_bf, part in reversed(rounded):
+                nc.vector.quantize_mx(out=out_codes[:, part].bitcast(FP8X4), scales=out_scales[:, part],
+                                      in_=res_bf[:].rearrange("p c t -> p (c t)"))
+            nc.sync.dma_start(out_words[:, cols], out_codes[:, cols].bitcast(I32))
         for q in range(4):
             eng = nc.scalar if q % 2 == 0 else nc.sync
             eng.dma_start(out_2[0, 4 * q : 4 * q + 4, :].bitcast(I32), out_scales[32 * q : 32 * q + 4, :].bitcast(I32))

from contextlib import ExitStack

import concourse.mybir as mybir

T, S, H, W = 2048, 256, 512, 128
P = 128
PACK = 4
WINDOW = 2 * S
HALF = S // 2
X_SPLIT = 768
PIECES = ((0, 128), (128, 128))
FLOPS = 3 * 2 * H * H * S

F32 = mybir.dt.float32
BF16 = mybir.dt.bfloat16
I32 = mybir.dt.int32
U32 = mybir.dt.uint32
U16 = mybir.dt.uint16
U8 = mybir.dt.uint8
FP8X4 = mybir.dt.float8_e4m3fn_x4
FP4X4 = mybir.dt.float4_e2m1fn_x4
ALU = mybir.AluOpType
ACT = mybir.ActivationFunctionType


def tile_picked_tietriebbondlap_none_po_kernel(tc, x_words, x_scales, w1_words, w1_scales, gn, w2_words, w2_scales,
        offs, n1, n2, n3, n4, n5, n6, out_0, out_1, out_2):
    nc = tc.nc
    with ExitStack() as ctx:
        pool = ctx.enter_context(tc.tile_pool(name="sbuf", bufs=1))
        psum = ctx.enter_context(tc.psum_pool(name="psum", bufs=1))

        def load_list(name, src):
            tl = pool.tile(list(src.shape), U16, name=name)
            nc.sync.dma_start(tl[:], src)
            return tl

        def zeroed_plane(name, width):
            tl = pool.tile([P, width], U8, name=name, align_bytes=64)
            nc.vector.memset(tl[:].bitcast(I32), 0)
            return tl

        def load_scale_rows(eng, tl, src, quadrants):
            for q in quadrants:
                eng.dma_start(tl[32 * q : 32 * q + 4, :].bitcast(I32), src[0, 4 * q : 4 * q + 4, :].bitcast(I32))

        def deal_words(raw):
            dealt = pool.tile([P, 2 * H], U8, name="dealt_words", align_bytes=64)
            nc.vector.tensor_copy(dealt[:].rearrange("p (t m e) -> p t m e", t=PACK, e=2),
                                  raw[:].rearrange("p (m t e) -> p t m e", t=PACK, e=2))
            return dealt

        def deal_words_on_scalar(raw):
            dealt = pool.tile([P, 2 * H], U8, name="dealt_words", align_bytes=64)
            nc.scalar.copy(dealt[:].bitcast(U16).rearrange("p (t m) -> p t m", t=PACK),
                           raw[:].bitcast(U16).rearrange("p (m t) -> p t m", t=PACK))
            return dealt

        def deal_scales(raw, pieces):
            dealt = pool.tile([P, H], U8, name="dealt_scales", align_bytes=64)
            for ts in pieces:
                nc.vector.tensor_copy(dealt[:].rearrange("p (t m) -> p t m", t=PACK)[:, ts, :],
                                      raw[:].rearrange("p (m t) -> p t m", t=PACK)[:, ts, :])
            return dealt

        ws_raw = zeroed_plane("ws_raw", H)
        xs_all = zeroed_plane("xs_all", T)
        ww_raw = pool.tile([P, 2 * H], U8, name="ww_raw", align_bytes=64)

        offs_t = load_list("offs_t", offs)
        nc.sync.dma_start(ww_raw[:].bitcast(I32), w1_words[0].bitcast(I32))
        load_scale_rows(nc.sync, ws_raw, w1_scales, range(1))
        xw_all = pool.tile([P, T], I32, name="xw_all", align_bytes=64)
        x_rows = x_words[0].rearrange("p c r -> p (c r)").bitcast(I32)
        nc.scalar.dma_start(xw_all[:, :X_SPLIT], x_rows[:, :X_SPLIT])
        nc.gpsimd.dma_start(xw_all[:, X_SPLIT:], x_rows[:, X_SPLIT:])
        load_scale_rows(nc.sync, xs_all, x_scales, range(4))
        load_scale_rows(nc.sync, ws_raw, w1_scales, range(1, 4))
        n1_t = load_list("n1_t", n1)
        n2_t = load_list("n2_t", n2)
        n3_t = load_list("n3_t", n3)
        n4_t = load_list("n4_t", n4)
        gain = pool.tile([P, PACK], F32, name="gain")
        nc.sync.dma_start(gain[:], gn.rearrange("(p t) o -> p (t o)", t=PACK))
        n6_t = load_list("n6_t", n6)
        n5_t = load_list("n5_t", n5)

        w1w = deal_words_on_scalar(ww_raw)

        xs = pool.tile([P, S], U8, name="xs", align_bytes=64)
        nc.vector.tensor_copy(xs[:], xs_all[:].indirect(offs_t[:]))
        xw = pool.tile([P, S], U32, name="xw", tag="xs_all", align_bytes=64)
        for h in range(2):
            nc.vector.tensor_copy(xw[:, HALF * h : HALF * (h + 1)],
                                  xw_all[:].bitcast(U32).indirect(offs_t[:, HALF // 16 * h : HALF // 16 * (h + 1)]))

        w1s = deal_scales(ws_raw, [slice(0, 1), slice(1, PACK)])
        nc.sync.dma_start(ww_raw[:].bitcast(I32), w2_words[0].bitcast(I32))
        load_scale_rows(nc.sync, ws_raw, w2_scales, range(4))

        def product(name, bank0, factor, words, scales, codes, code_scales):
            res = []
            for t in range(PACK):
                acc = psum.tile([P, S], F32, name="acc", tag="bank%d" % (bank0 + t))
                for cols in ([slice(0, HALF), slice(HALF, S)] if (name, t) == ("y", 0) else [slice(0, S)]):
                    nc.tensor.matmul_mx(
                        out=acc[:, cols],
                        lhsT=words[:, 2 * P * t : 2 * P * (t + 1)].bitcast(FP4X4),
                        lhsT_scale=scales[:, P * t : P * (t + 1)],
                        rhs=codes[:, cols].bitcast(FP8X4),
                        rhs_scale=code_scales[:, cols],
                        start=True, stop=True)
                win = pool.tile([P, WINDOW], F32, name="%s%d" % (name, t))
                nc.vector.tensor_scalar(win[:, :S], acc[:], factor, None, ALU.mult)
                res.append(win)
            return res

        def fetch(dst, win, lst):
            nc.scalar.activation(dst, win[:].indirect(lst), ACT.Copy)

        def quantize(name, grouped, tag):
            codes = pool.tile([P, S], U32, name=name + "_codes", tag=tag, align_bytes=64)
            scales = pool.tile([P, S], U8, name=name + "_scales", align_bytes=64)
            nc.vector.quantize_mx(out=codes[:].bitcast(FP8X4), scales=scales[:],
                                  in_=grouped[:].rearrange("p c t -> p (c t)"))
            return codes, scales

        y = product("y", 0, 1.0, w1w, w1s, xw, xs)

        ra, rb = [], []
        for t in range(PACK):
            pa = pool.tile([P, W], F32, name="pa%d" % t)
            pb = pool.tile([P, W], F32, name="pb%d" % t)
            fetch(pa[:], y[t], n1_t[:])
            fetch(pb[:], y[t], n2_t[:])
            ra.append(pool.tile([P, W], F32, name="ra%d" % t))
            rb.append(pool.tile([P, W], F32, name="rb%d" % t))
            nc.vector.tensor_tensor(ra[t][:], pa[:], pb[:], ALU.add)
            nc.vector.tensor_tensor(rb[t][:], pa[:], pb[:], ALU.mult)

        w2w = deal_words(ww_raw)
        w2s = deal_scales(ws_raw, [slice(0, PACK)])

        z2 = pool.tile([P, S, PACK], BF16, name="z2", align_bytes=64)
        for t in range(PACK):
            y3 = pool.tile([P, S], F32, name="y3_%d" % t)
            y4 = pool.tile([P, S], F32, name="y4_%d" % t)
            fetch(y3[:], y[t], n3_t[:])
            fetch(y4[:], y[t], n4_t[:])
            both = pool.tile([P, S], F32, name="both%d" % t)
            nc.vector.tensor_tensor(both[:], y3[:], y4[:], ALU.add)
            lap = pool.tile([P, S], F32, name="lap%d" % t)
            nc.vector.scalar_tensor_tensor(lap[:], both[:], 0.75, y[t][:, :S], ALU.mult, ALU.subtract)
            nc.vector.tensor_scalar(z2[:, :, t], lap[:], gain[:, t : t + 1], None, ALU.mult)
        b = product("b", PACK, 0.5, w2w, w2s, *quantize("z2", z2, "handed_on"))

        z = pool.tile([P, S, PACK], BF16, name="z", tag="handed_on", align_bytes=64)
        dt = [pool.tile([P, S], F32, name="dt%d" % t) for t in range(PACK)]
        nc.scalar.activation(dt[0][:].indirect(n1_t[:]), ra[0][:], ACT.Copy)
        for t in range(PACK):
            if t + 1 < PACK:
                nc.scalar.activation(dt[t + 1][:].indirect(n1_t[:]), ra[t + 1][:], ACT.Copy)
            nc.scalar.activation(dt[t][:].indirect(n2_t[:]), rb[t][:], ACT.Copy)
            nc.vector.tensor_scalar(z[:, :, t], dt[t][:], gain[:, t : t + 1], None, ALU.mult)
        a = product("a", 0, 0.5, w2w, w2s, *quantize("z", z, "z_codes"))

        gate = {}

        def make_gate(u, h, tag):
            gate[u, h] = pool.tile([P, 2, HALF], F32, name="gate", tag=tag)
            nc.scalar.activation(gate[u, h][:], bsum[:, 2 * u : 2 * u + 2, HALF * h : HALF * (h + 1)], ACT.Tanh)

        bsum = pool.tile([P, PACK, S], F32, name="bsum", tag="handed_on", align_bytes=64)
        for t in range(PACK):
            b6 = pool.tile([P, S], F32, name="b6_%d" % t)
            fetch(b6[:], b[t], n6_t[:])
            nc.vector.tensor_tensor(bsum[:, t, :], b6[:], b[t][:, :S], ALU.add)
            if t % 2 == 1:
                make_gate(t // 2, 0, "gate%d" % (t // 2))

        out_rows = out_0.rearrange("(p t) c -> p t c", t=PACK)
        out_codes = pool.tile([P, S], U32, name="out_codes", align_bytes=64)
        out_scales = pool.tile([P, S], U8, name="out_scales", align_bytes=64)
        out_words = out_1[0].rearrange("p c r -> p (c r)").bitcast(I32)
        res = pool.tile([P, PACK, S], F32, name="res")
        a5_first = pool.tile([P, PACK, HALF], F32, name="a5_first")
        a5_rest = pool.tile([P, PACK * HALF], F32, name="a5_rest", tag="b3")
        for h, (c0, n) in enumerate(PIECES):
            cols = slice(c0, c0 + n)
            a5 = a5_first[:] if h == 0 else a5_rest[:, PACK * (c0 - HALF) : PACK * (c0 - HALF + n)].rearrange("p (t c) -> p t c", t=PACK)
            asum = pool.tile([P, PACK, n], F32, name="asum%d" % h)
            for t in range(PACK):
                fetch(a5[:, t, :], a[t], n5_t[:, c0 // 16 : (c0 + n) // 16])
                nc.vector.tensor_tensor(asum[:, t, :], a5[:, t, :], a[t][:, cols], ALU.add)
                if h == 0:
                    nc.vector.scalar_tensor_tensor(res[:, t, cols], gate[t // 2, 0][:, t % 2, :], 1.0, asum[:, t, :], ALU.add, ALU.mult)
            if h == 1:
                for u in range(2):
                    ts = slice(2 * u, 2 * u + 2)
                    make_gate(u, 1, "a%d" % u)
                    nc.vector.scalar_tensor_tensor(res[:, ts, cols], gate[u, 1][:], 1.0, asum[:, ts, :], ALU.add, ALU.mult)
            nc.sync.dma_start(out_rows[:, :, cols], res[:, :, cols])
            if h == 0:
                shares = [(nc.vector.tensor_copy, cols)]
            else:
                shares = [(nc.vector.tensor_copy, slice(c0, c0 + n // 2)), (nc.scalar.copy, slice(c0 + n // 2, c0 + n))]
            rounded = []
            for copy, part in shares:
                res_bf = pool.tile([P, part.stop - part.start, PACK], BF16, name="res_bf%d" % part.start, align_bytes=64)
                copy(res_bf[:].rearrange("p (c i) t -> p c t i", i=4), res[:, :, part].rearrange("p t (c i) -> p c t i", i=4))
                rounded.append((res_bf, part))
            for res_bf, part in reversed(rounded):
                nc.vector.quantize_mx(out=out_codes[:, part].bitcast(FP8X4), scales=out_scales[:, part],
                                      in_=res_bf[:].rearrange("p c t -> p (c t)"))
            nc.sync.dma_start(out_words[:, cols], out_codes[:, cols].bitcast(I32))
        for q in range(4):
            eng = nc.scalar if q % 2 == 0 else nc.sync
            eng.dma_start(out_2[0, 4 * q : 4 * q + 4, :].bitcast(I32), out_scales[32 * q : 32 * q + 4, :].bitcast(I32))
